import numpy as np
import ml_dtypes


def mxq(x, axis, fmt="e4m3"):
    dtype, down = {"e4m3": (ml_dtypes.float8_e4m3fn, 7), "e5m2": (ml_dtypes.float8_e5m2, 14)}[fmt]
    v = np.moveaxis(np.asarray(x, np.float32).astype(ml_dtypes.bfloat16).astype(np.float64), axis, -1)
    blocks = v.reshape(v.shape[:-1] + (-1, 32))
    amax = np.abs(blocks).max(-1, keepdims=True)
    byte = np.maximum(np.where(amax > 0, np.frexp(amax)[1] - 1 + 127, 0) - down, 1)
    scale = np.exp2(byte - 127.0)
    codes = (blocks / scale).astype(np.float32).astype(dtype).astype(np.float64)
    return np.moveaxis((codes * scale).reshape(v.shape), -1, axis)


WIDE = False


def mx_kscale(k):
    if not WIDE:
        return np.ones(k)
    levels = np.array([10, -10, 5, -5, 0])
    if k % 512:
        return np.exp2(np.random.permutation(np.resize(levels, k // 32))).repeat(32)
    a = np.empty((k // 512, 16))
    for p in range(k // 512):
        a[p, :8] = np.random.permutation(np.resize(levels, 8))
        for g in range(8):
            far = levels[np.abs(levels - a[p, g]) >= 10]
            a[p, g + 8] = far[np.random.randint(len(far))]
    return np.exp2(a.ravel()).repeat(32)


def f64(x):
    return np.asarray(x).astype(np.float64)


def striped(idx):
    return np.tile(np.asarray(idx).reshape(-1, 16).T, (8, 1)).astype(np.uint16)


def unstriped(offs):
    return offs[:16].T.reshape(-1).astype(np.int64)


E2M1 = np.array([0.0, 0.5, 1.0, 1.5, 2.0, 3.0, 4.0, 6.0, -0.0, -0.5, -1.0, -1.5, -2.0, -3.0, -4.0, -6.0])


def pack_weight(w, fmt):
    k, n = w.shape
    w = f64(np.asarray(w, np.float32).astype(ml_dtypes.bfloat16)).reshape(k // 32, 32, n)
    amax = np.abs(w).max(1)
    if fmt == "e4m3":
        byte = np.frexp(amax)[1] - 1 + 127 - 7
    else:
        mant, ex = np.frexp(amax / 6.0)
        byte = np.where(mant > 0.5, ex, ex - 1) + 127
    byte = np.clip(np.where(amax > 0, byte, 1), 1, 254)
    scaled = (w * np.exp2(127.0 - byte)[:, None, :]).reshape(k, n).astype(np.float32)
    by_word = np.ascontiguousarray(scaled.reshape(k // 512, 128, 4, n).transpose(0, 1, 3, 2))
    if fmt == "e4m3":
        words = by_word.astype(ml_dtypes.float8_e4m3fn).view(np.uint8)
    else:
        c = by_word.astype(ml_dtypes.float4_e2m1fn).view(np.uint8) & 0xF
        words = (c[..., 0::2] | (c[..., 1::2] << 4)).reshape(k // 512, 128, 2 * n)
    return np.ascontiguousarray(words), np.ascontiguousarray(byte.astype(np.uint8).reshape(k // 512, 16, n))


def unpack_weight(words, scales, fmt):
    g, _, n = scales.shape
    words = np.ascontiguousarray(words).reshape(g, 128, n, -1)
    if fmt == "e4m3":
        vals = words.view(ml_dtypes.float8_e4m3fn).astype(np.float64)
    else:
        nib = np.empty((g, 128, n, 4), np.uint8)
        nib[..., 0::2] = words & 0xF
        nib[..., 1::2] = words >> 4
        vals = E2M1[nib]
    vals = vals * np.repeat(np.exp2(scales.astype(np.float64) - 127.0), 8, axis=1)[..., None]
    return vals.transpose(0, 1, 3, 2).reshape(g * 512, n)


D, E, T, I, Q = 512, 512, 2048, 512, 128


def setup_inputs():
    n = np.random.standard_normal
    idx = np.random.permutation(T)[:I]
    fd = mx_kscale(D)
    fe = mx_kscale(E)
    keysp = pack_weight(n((D, T)) / fd[:, None], "e4m3")
    valsp = pack_weight(n((E, T)) / fe[:, None], "e4m3")
    return {
        "query": (n((D, Q)) * 0.4 / np.sqrt(D) * fd[:, None]).astype(np.float32),
        "query2": (n((D, Q)) * 0.6 / np.sqrt(D) * fd[:, None]).astype(np.float32),
        "keys_words": keysp[0],
        "keys_scales": keysp[1],
        "l1": (np.random.uniform(6.2, 6.5, (Q, 1))).astype(np.float32),
        "l2": (np.random.uniform(6.2, 6.5, (Q, 1))).astype(np.float32),
        "floor": (np.random.uniform(0.0005, 0.002, (Q, 1))).astype(np.float32),
        "gout": (n((E, Q)) * 1 / np.sqrt(E) * fe[:, None]).astype(np.float32),
        "vals_words": valsp[0],
        "vals_scales": valsp[1],
        "size": (np.random.uniform(0.5, 2.0, (1, I))).astype(np.float32),
        "dquery2": (n((D, Q)) * 1.0 / np.sqrt(D) * fd[:, None]).astype(np.float32),
        "base": (0.5 * n((Q, T))).astype(np.float32),
        "offs": striped(idx),
    }


def reference(query, query2, keys_words, keys_scales, l1, l2, floor, gout, vals_words, vals_scales, size, dquery2, base, offs):
    idx = unstriped(offs)
    keysu = unpack_weight(keys_words, keys_scales, "e4m3")
    valsu = unpack_weight(vals_words, vals_scales, "e4m3")
    queryq = mxq(f64(query), 0, "e4m3")
    keysidxg = keysu[:, idx]
    a = queryq.T @ keysidxg
    query2q = mxq(f64(query2), 0, "e4m3")
    b = query2q.T @ keysidxg
    dquery2q = mxq(f64(dquery2), 0, "e4m3")
    tb = dquery2q.T @ keysidxg
    pa = np.exp(a - f64(l1))
    pb = np.exp(b - f64(l2))
    goutq = mxq(f64(gout), 0, "e4m3")
    valsidxg = valsu[:, idx]
    c0 = goutq.T @ valsidxg
    dpb = c0 * f64(size) * pa / np.square(pb + f64(floor)) * (-1.0)
    tpb = tb * pb
    tdpb = tpb * (pb + f64(floor)) * 2.0 * c0 * f64(size) * pa / np.square(np.square(pb + f64(floor))) * (-1.0) * (-1.0)
    tdb = tdpb * pb + tpb * dpb
    gs = tdb * 512.0
    gf = np.zeros((Q, T))
    gf[:, idx] = gs
    y = f64(base) + gf
    return y

@@ -1,0 +1,178 @@
+from contextlib import ExitStack
+
+import concourse.mybir as mybir
+from concourse.masks import make_identity
+
+D, E, T, I, Q = 512, 512, 2048, 512, 128
+FLOPS = 4 * 2 * D * Q * I
+
+F32 = mybir.dt.float32
+BF16 = mybir.dt.bfloat16
+I32 = mybir.dt.int32
+U32 = mybir.dt.uint32
+U16 = mybir.dt.uint16
+U8 = mybir.dt.uint8
+FP8X4 = mybir.dt.float8_e4m3fn_x4
+ALU = mybir.AluOpType
+ACT = mybir.ActivationFunctionType
+
+P = 128
+PACK = 4
+VALS_ROW = 4
+OUT_CHUNK = 512
+
+
+def tile_attend_hvclippedratio_b_s_kernel(
+    tc, query, query2, keys_words, keys_scales, l1, l2, floor, gout, vals_words, vals_scales, size, dquery2, base, offs, out
+):
+    nc = tc.nc
+    with ExitStack() as ctx:
+        sb = ctx.enter_context(tc.tile_pool(name="sb", bufs=1))
+        ps = ctx.enter_context(tc.psum_pool(name="ps", bufs=1))
+
+        def tile(name, cols, dtype):
+            return sb.tile([P, cols], dtype, name=name, align_bytes=64)
+
+        offsets = sb.tile([P, I // 16], U16, name="offsets")
+        nc.sync.dma_start(offsets[:], offs)
+
+        key_bytes = tile("key_bytes", T, U8)
+        val_bytes = tile("val_bytes", T, U8)
+        nc.vector.memset(key_bytes[:].bitcast(I32), 0)
+        nc.vector.memset(val_bytes[:].bitcast(I32), 0)
+        placed = tile("placed", T, F32)
+        nc.vector.memset(placed[:], 0.0)
+
+        def load_rows(name, src):
+            raw = sb.tile([P, PACK, Q], F32, name=name + "_raw")
+            nc.sync.dma_start(raw[:], src.rearrange("(p j) w -> p j w", j=PACK))
+            return raw
+
+        def load_scale_bytes(queue, dst, src, first):
+            for quad in range(4):
+                rows = slice(32 * quad + first, 32 * quad + first + 4)
+                queue.dma_start(dst[rows, :].bitcast(I32), src[0, 4 * quad : 4 * quad + 4, :].bitcast(I32))
+
+        def load_words(name, src):
+            words = tile(name, T, U32)
+            nc.sync.dma_start(words[:].bitcast(I32), src[0].rearrange("p n t -> p (n t)").bitcast(I32))
+            return words
+
+        def load_column(name, src):
+            col = sb.tile([P, 1], F32, name=name)
+            nc.sync.dma_start(col[:], src)
+            return col
+
+        q2_raw = load_rows("q2", query2)
+        q1_raw = load_rows("q1", query)
+        load_scale_bytes(nc.sync, key_bytes, keys_scales, 0)
+        key_words = load_words("key_words", keys_words)
+        l2_col = load_column("l2_col", l2)
+        floor_col = load_column("floor_col", floor)
+        l1_col = load_column("l1_col", l1)
+        size_cols = sb.tile([P, PACK], F32, name="size_cols")
+        nc.sync.dma_start(size_cols[:], size.rearrange("o (p j) -> (o p) j", j=PACK))
+        dq_raw = load_rows("dq", dquery2)
+        go_raw = load_rows("go", gout)
+        load_scale_bytes(nc.sync, val_bytes, vals_scales, VALS_ROW)
+        val_words = load_words("val_words", vals_words)
+        base_sb = tile("base_sb", T, F32)
+        nc.sync.dma_start(base_sb[:], base)
+
+        ident = tile("ident", P, F32)
+        make_identity(nc, ident[:])
+
+        neg_l2 = sb.tile([P, 1], F32, name="neg_l2")
+        nc.scalar.activation(neg_l2[:], l2_col[:], ACT.Copy, scale=-1.0)
+        neg_l12 = sb.tile([P, 1], F32, name="neg_l12")
+        nc.scalar.activation(neg_l12[:], l1_col[:], ACT.Identity, bias=neg_l2[:], scale=-1.0)
+        floor_sq = sb.tile([P, 1], F32, name="floor_sq")
+        nc.scalar.activation(floor_sq[:], floor_col[:], ACT.Square)
+
+        size_ps = ps.tile([P, PACK, P], F32, name="size_ps")
+        for j in range(PACK):
+            nc.tensor.transpose(size_ps[:, j, :], size_cols[:, j : j + 1].to_broadcast([P, P]), ident[:])
+
+        def interleave(name, raw, on_scalar):
+            grouped = sb.tile([P, Q, PACK], BF16, name=name + "_bf", align_bytes=64)
+            src = raw[:].rearrange("p j w -> p w j")
+            if on_scalar:
+                nc.scalar.copy(grouped[:], src)
+            else:
+                nc.vector.tensor_copy(grouped[:], src)
+            return grouped
+
+        def quantize(name, grouped):
+            codes = tile(name + "_codes", Q, U32)
+            scales = tile(name + "_scales", Q, U8)
+            nc.vector.quantize_mx(out=codes[:].bitcast(FP8X4), scales=scales[:], in_=grouped[:].rearrange("p w j -> p (w j)"))
+            return codes, scales
+
+        def gather(name, window, dtype):
+            picked = tile(name, I, dtype)
+            nc.vector.tensor_copy(picked[:], window[:].indirect(offsets[:]))
+            return picked
+
+        def product(acc, rows, words, planes, start, stop):
+            nc.tensor.matmul_mx(
+                out=acc[:], lhsT=rows[0][:].bitcast(FP8X4), lhsT_scale=rows[1][:],
+                rhs=words[:].bitcast(FP8X4), rhs_scale=planes, start=start, stop=stop,
+            )
+
+        q2_bf = interleave("q2", q2_raw, False)
+        q1_bf = interleave("q1", q1_raw, True)
+        key_sc = gather("key_sc", key_bytes, U8)
+        q2_mx = quantize("q2", q2_bf)
+        q1_mx = quantize("q1", q1_bf)
+        key_w = gather("key_w", key_words, U32)
+
+        b_ps = ps.tile([P, I], F32, name="b_ps")
+        product(b_ps, q2_mx, key_w, key_sc[:], True, True)
+        ab_ps = ps.tile([P, I], F32, name="ab_ps")
+        product(ab_ps, q2_mx, key_w, key_sc[:], True, False)
+        product(ab_ps, q1_mx, key_w, key_sc[:], False, True)
+
+        pb = tile("pb", I, F32)
+        nc.scalar.activation(pb[:], b_ps[:], ACT.Exp, bias=neg_l2[:])
+        den_sq = tile("den_sq", I, F32)
+        nc.scalar.activation(den_sq[:], pb[:], ACT.Square, bias=floor_col[:])
+        pab = tile("pab", I, F32)
+        nc.scalar.activation(pab[:], ab_ps[:], ACT.Exp, bias=neg_l12[:])
+        pb_sq = tile("pb_sq", I, F32)
+        nc.scalar.activation(pb_sq[:], pb[:], ACT.Square)
+        inv_abs = tile("inv_abs", I, F32)
+        nc.scalar.activation(inv_abs[:], den_sq[:], ACT.Abs_reciprocal_sqrt)
+        inv_sq = tile("inv_sq", I, F32)
+        nc.scalar.activation(inv_sq[:], inv_abs[:], ACT.Square)
+
+        dq_bf = interleave("dq", dq_raw, False)
+        go_bf = interleave("go", go_raw, False)
+        dq_mx = quantize("dq", dq_bf)
+        go_mx = quantize("go", go_bf)
+        val_sc = gather("val_sc", val_bytes, U8)
+        tb_ps = ps.tile([P, I], F32, name="tb_ps")
+        product(tb_ps, dq_mx, key_w, key_sc[:], True, True)
+
+        m1 = tile("m1", I, F32)
+        nc.vector.tensor_tensor(m1[:], tb_ps[:], pab[:], ALU.mult)
+        m2 = tile("m2", I, F32)
+        nc.vector.scalar_tensor_tensor(
+            m2[:].rearrange("p (n j) -> p n j", j=PACK), size_ps[:].rearrange("p j n -> p n j"), 512.0,
+            m1[:].rearrange("p (n j) -> p n j", j=PACK), ALU.mult, ALU.mult,
+        )
+        val_w = gather("val_w", val_words, U32)
+        c0_ps = ps.tile([P, I], F32, name="c0_ps")
+        product(c0_ps, go_mx, val_w, val_sc[VALS_ROW:P, :], True, True)
+        m3 = tile("m3", I, F32)
+        nc.vector.scalar_tensor_tensor(m3[:], pb_sq[:], floor_sq[:], m2[:], ALU.subtract, ALU.mult)
+        m4 = tile("m4", I, F32)
+        nc.vector.tensor_tensor(m4[:], c0_ps[:], m3[:], ALU.mult)
+        m5 = tile("m5", I, F32)
+        nc.vector.tensor_tensor(m5[:], m4[:], inv_sq[:], ALU.mult)
+        nc.vector.tensor_tensor(placed[:].indirect(offsets[:]), m5[:], inv_sq[:], ALU.mult)
+
+        for c in range(T // OUT_CHUNK):
+            cols = slice(c * OUT_CHUNK, (c + 1) * OUT_CHUNK)
+            res = tile("res%d" % c, OUT_CHUNK, F32)
+            nc.vector.tensor_tensor(res[:], placed[:, cols], base_sb[:, cols], ALU.add)
+            nc.sync.dma_start(out[:, cols], res[:])

@@ -19,7 +19,7 @@ ACT = mybir.ActivationFunctionType
 P = 128
 PACK = 4
 VALS_ROW = 4
-OUT_CHUNK = 512
+OUT_WIDTHS = (640, 640, 512, 256)
 
 
 def tile_attend_hvclippedratio_b_s_kernel(
@@ -30,8 +30,8 @@ def tile_attend_hvclippedratio_b_s_kernel(
         sb = ctx.enter_context(tc.tile_pool(name="sb", bufs=1))
         ps = ctx.enter_context(tc.psum_pool(name="ps", bufs=1))
 
-        def tile(name, cols, dtype):
-            return sb.tile([P, cols], dtype, name=name, align_bytes=64)
+        def tile(name, cols, dtype, tag=None):
+            return sb.tile([P, cols], dtype, name=name, tag=tag or name, align_bytes=64)
 
         offsets = sb.tile([P, I // 16], U16, name="offsets")
         nc.sync.dma_start(offsets[:], offs)
@@ -60,38 +60,36 @@ def tile_attend_hvclippedratio_b_s_kernel(
 
         def load_column(name, src):
             col = sb.tile([P, 1], F32, name=name)
-            nc.sync.dma_start(col[:], src)
+            nc.gpsimd.dma_start(col[:], src)
             return col
 
         q2_raw = load_rows("q2", query2)
-        q1_raw = load_rows("q1", query)
         load_scale_bytes(nc.sync, key_bytes, keys_scales, 0)
         key_words = load_words("key_words", keys_words)
+        q1_raw = load_rows("q1", query)
+        dq_raw = load_rows("dq", dquery2)
+        load_scale_bytes(nc.sync, val_bytes, vals_scales, VALS_ROW)
+        val_words = load_words("val_words", vals_words)
+        go_raw = load_rows("go", gout)
+        base_sb = tile("base_sb", T, F32)
+        nc.sync.dma_start(base_sb[:], base)
+
         l2_col = load_column("l2_col", l2)
         floor_col = load_column("floor_col", floor)
         l1_col = load_column("l1_col", l1)
         size_cols = sb.tile([P, PACK], F32, name="size_cols")
-        nc.sync.dma_start(size_cols[:], size.rearrange("o (p j) -> (o p) j", j=PACK))
-        dq_raw = load_rows("dq", dquery2)
-        go_raw = load_rows("go", gout)
-        load_scale_bytes(nc.sync, val_bytes, vals_scales, VALS_ROW)
-        val_words = load_words("val_words", vals_words)
-        base_sb = tile("base_sb", T, F32)
-        nc.sync.dma_start(base_sb[:], base)
+        nc.gpsimd.dma_start(size_cols[:], size.rearrange("o (p j) -> (o p) j", j=PACK))
 
         ident = tile("ident", P, F32)
         make_identity(nc, ident[:])
 
         neg_l2 = sb.tile([P, 1], F32, name="neg_l2")
         nc.scalar.activation(neg_l2[:], l2_col[:], ACT.Copy, scale=-1.0)
-        neg_l12 = sb.tile([P, 1], F32, name="neg_l12")
+        neg_l12 = tile("neg_l12", 1, F32)
         nc.scalar.activation(neg_l12[:], l1_col[:], ACT.Identity, bias=neg_l2[:], scale=-1.0)
         floor_sq = sb.tile([P, 1], F32, name="floor_sq")
         nc.scalar.activation(floor_sq[:], floor_col[:], ACT.Square)
 
-        size_ps = ps.tile([P, PACK, P], F32, name="size_ps")
-        for j in range(PACK):
-            nc.tensor.transpose(size_ps[:, j, :], size_cols[:, j : j + 1].to_broadcast([P, P]), ident[:])
 
         def interleave(name, raw, on_scalar):
             grouped = sb.tile([P, Q, PACK], BF16, name=name + "_bf", align_bytes=64)
@@ -108,71 +106,78 @@ def tile_attend_hvclippedratio_b_s_kernel(
             nc.vector.quantize_mx(out=codes[:].bitcast(FP8X4), scales=scales[:], in_=grouped[:].rearrange("p w j -> p (w j)"))
             return codes, scales
 
-        def gather(name, window, dtype):
-            picked = tile(name, I, dtype)
-            nc.vector.tensor_copy(picked[:], window[:].indirect(offsets[:]))
+        def gather(name, window, dtype, slots):
+            picked = tile(name, slots.stop - slots.start, dtype)
+            nc.vector.tensor_copy(picked[:], window[:].indirect(offsets[:, slots.start // 16 : slots.stop // 16]))
             return picked
 
         def product(acc, rows, words, planes, start, stop):
             nc.tensor.matmul_mx(
-                out=acc[:], lhsT=rows[0][:].bitcast(FP8X4), lhsT_scale=rows[1][:],
+                out=acc, lhsT=rows[0][:].bitcast(FP8X4), lhsT_scale=rows[1][:],
                 rhs=words[:].bitcast(FP8X4), rhs_scale=planes, start=start, stop=stop,
             )
 
-        q2_bf = interleave("q2", q2_raw, False)
-        q1_bf = interleave("q1", q1_raw, True)
-        key_sc = gather("key_sc", key_bytes, U8)
-        q2_mx = quantize("q2", q2_bf)
-        q1_mx = quantize("q1", q1_bf)
-        key_w = gather("key_w", key_words, U32)
+        every = slice(0, I)
+        halves = [slice(0, I // 2), slice(I // 2, I)]
 
-        b_ps = ps.tile([P, I], F32, name="b_ps")
-        product(b_ps, q2_mx, key_w, key_sc[:], True, True)
-        ab_ps = ps.tile([P, I], F32, name="ab_ps")
-        product(ab_ps, q2_mx, key_w, key_sc[:], True, False)
-        product(ab_ps, q1_mx, key_w, key_sc[:], False, True)
+        q2_bf = interleave("q2", q2_raw, False)
+        key_sc = gather("key_sc", key_bytes, U8, every)
+        q2_mx = quantize("q2", q2_bf)
+        key_w = [gather("key_w%d" % h, key_words, U32, slots) for h, slots in enumerate(halves)]
+        q1_mx = quantize("q1", interleave("q1", q1_raw, True))
 
         pb = tile("pb", I, F32)
-        nc.scalar.activation(pb[:], b_ps[:], ACT.Exp, bias=neg_l2[:])
         den_sq = tile("den_sq", I, F32)
-        nc.scalar.activation(den_sq[:], pb[:], ACT.Square, bias=floor_col[:])
-        pab = tile("pab", I, F32)
-        nc.scalar.activation(pab[:], ab_ps[:], ACT.Exp, bias=neg_l12[:])
+        for h, slots in enumerate(halves):
+            b_ps = ps.tile([P, I // 2], F32, name="b_ps%d" % h)
+            product(b_ps[:], q2_mx, key_w[h], key_sc[:, slots], True, True)
+            nc.scalar.activation(pb[:, slots], b_ps[:], ACT.Exp, bias=neg_l2[:])
+            nc.scalar.activation(den_sq[:, slots], pb[:, slots], ACT.Square, bias=floor_col[:])
+        ab_ps = ps.tile([P, I], F32, name="ab_ps")
+        for h, slots in enumerate(halves):
+            product(ab_ps[:, slots], q2_mx, key_w[h], key_sc[:, slots], True, False)
+            product(ab_ps[:, slots], q1_mx, key_w[h], key_sc[:, slots], False, True)
         pb_sq = tile("pb_sq", I, F32)
         nc.scalar.activation(pb_sq[:], pb[:], ACT.Square)
-        inv_abs = tile("inv_abs", I, F32)
+        pab = tile("pab", I, F32)
+        nc.scalar.activation(pab[:], ab_ps[:], ACT.Exp, bias=neg_l12[:])
+        size_ps = ps.tile([P, PACK, P], F32, name="size_ps", tag="ab_ps")
+        for j in range(PACK):
+            nc.tensor.transpose(size_ps[:, j, :], size_cols[:, j : j + 1].to_broadcast([P, P]), ident[:])
+        inv_abs = tile("inv_abs", I, F32, tag="neg_l12")
         nc.scalar.activation(inv_abs[:], den_sq[:], ACT.Abs_reciprocal_sqrt)
         inv_sq = tile("inv_sq", I, F32)
         nc.scalar.activation(inv_sq[:], inv_abs[:], ACT.Square)
 
-        dq_bf = interleave("dq", dq_raw, False)
-        go_bf = interleave("go", go_raw, False)
-        dq_mx = quantize("dq", dq_bf)
-        go_mx = quantize("go", go_bf)
-        val_sc = gather("val_sc", val_bytes, U8)
+        dq_mx = quantize("dq", interleave("dq", dq_raw, False))
         tb_ps = ps.tile([P, I], F32, name="tb_ps")
-        product(tb_ps, dq_mx, key_w, key_sc[:], True, True)
-
-        m1 = tile("m1", I, F32)
-        nc.vector.tensor_tensor(m1[:], tb_ps[:], pab[:], ALU.mult)
-        m2 = tile("m2", I, F32)
-        nc.vector.scalar_tensor_tensor(
-            m2[:].rearrange("p (n j) -> p n j", j=PACK), size_ps[:].rearrange("p j n -> p n j"), 512.0,
-            m1[:].rearrange("p (n j) -> p n j", j=PACK), ALU.mult, ALU.mult,
-        )
-        val_w = gather("val_w", val_words, U32)
+        for h, slots in enumerate(halves):
+            product(tb_ps[:, slots], dq_mx, key_w[h], key_sc[:, slots], True, True)
+        val_sc = gather("val_sc", val_bytes, U8, every)
+        val_w = gather("val_w", val_words, U32, every)
+        go_mx = quantize("go", interleave("go", go_raw, False))
         c0_ps = ps.tile([P, I], F32, name="c0_ps")
-        product(c0_ps, go_mx, val_w, val_sc[VALS_ROW:P, :], True, True)
-        m3 = tile("m3", I, F32)
-        nc.vector.scalar_tensor_tensor(m3[:], pb_sq[:], floor_sq[:], m2[:], ALU.subtract, ALU.mult)
-        m4 = tile("m4", I, F32)
-        nc.vector.tensor_tensor(m4[:], c0_ps[:], m3[:], ALU.mult)
-        m5 = tile("m5", I, F32)
-        nc.vector.tensor_tensor(m5[:], m4[:], inv_sq[:], ALU.mult)
-        nc.vector.tensor_tensor(placed[:].indirect(offsets[:]), m5[:], inv_sq[:], ALU.mult)
+        product(c0_ps[:], go_mx, val_w, val_sc[VALS_ROW:P, :], True, True)
 
-        for c in range(T // OUT_CHUNK):
-            cols = slice(c * OUT_CHUNK, (c + 1) * OUT_CHUNK)
-            res = tile("res%d" % c, OUT_CHUNK, F32)
+        m1 = tile("m1", I, F32, tag="go_bf")
+        nc.vector.scalar_tensor_tensor(m1[:], tb_ps[:], 512.0, pab[:], ALU.mult, ALU.mult)
+        n1 = tile("n1", I, F32, tag="val_words")
+        nc.vector.scalar_tensor_tensor(
+            n1[:].rearrange("p (n j) -> p n j", j=PACK), pb_sq[:].rearrange("p (n j) -> p n j", j=PACK), floor_sq[:],
+            size_ps[:].rearrange("p j n -> p n j"), ALU.subtract, ALU.mult,
+        )
+        m2 = tile("m2", I, F32)
+        nc.vector.tensor_tensor(m2[:], c0_ps[:], m1[:], ALU.mult)
+        n2 = tile("n2", I, F32, tag="go_bf")
+        nc.vector.tensor_tensor(n2[:], n1[:], inv_sq[:], ALU.mult)
+        m3 = tile("m3", I, F32)
+        nc.vector.tensor_tensor(m3[:], m2[:], inv_sq[:], ALU.mult)
+        nc.vector.tensor_tensor(placed[:].indirect(offsets[:]), m3[:], n2[:], ALU.mult)
+
+        first = 0
+        for c, width in enumerate(OUT_WIDTHS):
+            cols = slice(first, first + width)
+            first = first + width
+            res = tile("res%d" % c, width, F32)
             nc.vector.tensor_tensor(res[:], placed[:, cols], base_sb[:, cols], ALU.add)
             nc.sync.dma_start(out[:, cols], res[:])

@@ -19,7 +19,7 @@ ACT = mybir.ActivationFunctionType
 P = 128
 PACK = 4
 VALS_ROW = 4
-OUT_WIDTHS = (640, 640, 512, 256)
+OUT_WIDTHS = (512, 512, 512, 512)
 
 
 def tile_attend_hvclippedratio_b_s_kernel(
@@ -38,8 +38,8 @@ def tile_attend_hvclippedratio_b_s_kernel(
 
         key_bytes = tile("key_bytes", T, U8)
         val_bytes = tile("val_bytes", T, U8)
-        nc.vector.memset(key_bytes[:].bitcast(I32), 0)
-        nc.vector.memset(val_bytes[:].bitcast(I32), 0)
+        nc.gpsimd.memset(key_bytes[:].bitcast(I32), 0)
+        nc.gpsimd.memset(val_bytes[:].bitcast(I32), 0)
         placed = tile("placed", T, F32)
         nc.vector.memset(placed[:], 0.0)
 
@@ -48,10 +48,10 @@ def tile_attend_hvclippedratio_b_s_kernel(
             nc.sync.dma_start(raw[:], src.rearrange("(p j) w -> p j w", j=PACK))
             return raw
 
-        def load_scale_bytes(queue, dst, src, first):
-            for quad in range(4):
+        def load_scale_bytes(dst, src, first, quads):
+            for quad in quads:
                 rows = slice(32 * quad + first, 32 * quad + first + 4)
-                queue.dma_start(dst[rows, :].bitcast(I32), src[0, 4 * quad : 4 * quad + 4, :].bitcast(I32))
+                nc.sync.dma_start(dst[rows, :].bitcast(I32), src[0, 4 * quad : 4 * quad + 4, :].bitcast(I32))
 
         def load_words(name, src):
             words = tile(name, T, U32)
@@ -59,45 +59,43 @@ def tile_attend_hvclippedratio_b_s_kernel(
             return words
 
         def load_column(name, src):
-            col = sb.tile([P, 1], F32, name=name)
-            nc.gpsimd.dma_start(col[:], src)
+            col = tile(name, 1, F32)
+            nc.sync.dma_start(col[:], src)
             return col
 
         q2_raw = load_rows("q2", query2)
-        load_scale_bytes(nc.sync, key_bytes, keys_scales, 0)
-        key_words = load_words("key_words", keys_words)
         q1_raw = load_rows("q1", query)
-        dq_raw = load_rows("dq", dquery2)
-        load_scale_bytes(nc.sync, val_bytes, vals_scales, VALS_ROW)
-        val_words = load_words("val_words", vals_words)
-        go_raw = load_rows("go", gout)
-        base_sb = tile("base_sb", T, F32)
-        nc.sync.dma_start(base_sb[:], base)
-
+        load_scale_bytes(key_bytes, keys_scales, 0, range(4))
+        key_words = load_words("key_words", keys_words)
         l2_col = load_column("l2_col", l2)
         floor_col = load_column("floor_col", floor)
-        l1_col = load_column("l1_col", l1)
         size_cols = sb.tile([P, PACK], F32, name="size_cols")
-        nc.gpsimd.dma_start(size_cols[:], size.rearrange("o (p j) -> (o p) j", j=PACK))
+        nc.sync.dma_start(size_cols[:], size.rearrange("o (p j) -> (o p) j", j=PACK))
+        l1_col = load_column("l1_col", l1)
+        dq_raw = load_rows("dq", dquery2)
+        go_raw = load_rows("go", gout)
+        load_scale_bytes(val_bytes, vals_scales, VALS_ROW, range(4))
+        val_words = load_words("val_words", vals_words)
+        base_sb = tile("base_sb", T, F32)
+        nc.sync.dma_start(base_sb[:], base)
 
         ident = tile("ident", P, F32)
         make_identity(nc, ident[:])
 
         neg_l2 = sb.tile([P, 1], F32, name="neg_l2")
         nc.scalar.activation(neg_l2[:], l2_col[:], ACT.Copy, scale=-1.0)
-        neg_l12 = tile("neg_l12", 1, F32)
-        nc.scalar.activation(neg_l12[:], l1_col[:], ACT.Identity, bias=neg_l2[:], scale=-1.0)
         floor_sq = sb.tile([P, 1], F32, name="floor_sq")
         nc.scalar.activation(floor_sq[:], floor_col[:], ACT.Square)
 
 
         def interleave(name, raw, on_scalar):
             grouped = sb.tile([P, Q, PACK], BF16, name=name + "_bf", align_bytes=64)
-            src = raw[:].rearrange("p j w -> p w j")
+            dst = grouped[:].rearrange("p (c i) j -> p c j i", i=4)
+            src = raw[:].rearrange("p j (c i) -> p c j i", i=4)
             if on_scalar:
-                nc.scalar.copy(grouped[:], src)
+                nc.scalar.copy(dst, src)
             else:
-                nc.vector.tensor_copy(grouped[:], src)
+                nc.vector.tensor_copy(dst, src)
             return grouped
 
         def quantize(name, grouped):
@@ -121,10 +119,11 @@ def tile_attend_hvclippedratio_b_s_kernel(
         halves = [slice(0, I // 2), slice(I // 2, I)]
 
         q2_bf = interleave("q2", q2_raw, False)
+        q1_bf = interleave("q1", q1_raw, True)
         key_sc = gather("key_sc", key_bytes, U8, every)
         q2_mx = quantize("q2", q2_bf)
+        q1_mx = quantize("q1", q1_bf)
         key_w = [gather("key_w%d" % h, key_words, U32, slots) for h, slots in enumerate(halves)]
-        q1_mx = quantize("q1", interleave("q1", q1_raw, True))
 
         pb = tile("pb", I, F32)
         den_sq = tile("den_sq", I, F32)
@@ -139,40 +138,44 @@ def tile_attend_hvclippedratio_b_s_kernel(
             product(ab_ps[:, slots], q1_mx, key_w[h], key_sc[:, slots], False, True)
         pb_sq = tile("pb_sq", I, F32)
         nc.scalar.activation(pb_sq[:], pb[:], ACT.Square)
+        neg_l12 = tile("neg_l12", 1, F32)
+        nc.scalar.activation(neg_l12[:], l1_col[:], ACT.Identity, bias=neg_l2[:], scale=-1.0)
         pab = tile("pab", I, F32)
         nc.scalar.activation(pab[:], ab_ps[:], ACT.Exp, bias=neg_l12[:])
-        size_ps = ps.tile([P, PACK, P], F32, name="size_ps", tag="ab_ps")
+        size_ps = ps.tile([P, PACK, P], F32, name="size_ps", tag="b_ps1")
         for j in range(PACK):
             nc.tensor.transpose(size_ps[:, j, :], size_cols[:, j : j + 1].to_broadcast([P, P]), ident[:])
         inv_abs = tile("inv_abs", I, F32, tag="neg_l12")
         nc.scalar.activation(inv_abs[:], den_sq[:], ACT.Abs_reciprocal_sqrt)
         inv_sq = tile("inv_sq", I, F32)
         nc.scalar.activation(inv_sq[:], inv_abs[:], ACT.Square)
+        inv_4th = tile("inv_4th", I, F32)
+        nc.scalar.activation(inv_4th[:], inv_sq[:], ACT.Square)
 
-        dq_mx = quantize("dq", interleave("dq", dq_raw, False))
+        dq_bf = interleave("dq", dq_raw, False)
+        go_bf = interleave("go", go_raw, False)
+        dq_mx = quantize("dq", dq_bf)
+        go_mx = quantize("go", go_bf)
+        val_sc = gather("val_sc", val_bytes, U8, every)
         tb_ps = ps.tile([P, I], F32, name="tb_ps")
         for h, slots in enumerate(halves):
             product(tb_ps[:, slots], dq_mx, key_w[h], key_sc[:, slots], True, True)
-        val_sc = gather("val_sc", val_bytes, U8, every)
         val_w = gather("val_w", val_words, U32, every)
-        go_mx = quantize("go", interleave("go", go_raw, False))
         c0_ps = ps.tile([P, I], F32, name="c0_ps")
         product(c0_ps[:], go_mx, val_w, val_sc[VALS_ROW:P, :], True, True)
 
-        m1 = tile("m1", I, F32, tag="go_bf")
+        m1 = tile("m1", I, F32)
         nc.vector.scalar_tensor_tensor(m1[:], tb_ps[:], 512.0, pab[:], ALU.mult, ALU.mult)
-        n1 = tile("n1", I, F32, tag="val_words")
+        n1 = tile("n1", I, F32, tag="val_bytes")
         nc.vector.scalar_tensor_tensor(
             n1[:].rearrange("p (n j) -> p n j", j=PACK), pb_sq[:].rearrange("p (n j) -> p n j", j=PACK), floor_sq[:],
             size_ps[:].rearrange("p j n -> p n j"), ALU.subtract, ALU.mult,
         )
-        m2 = tile("m2", I, F32)
-        nc.vector.tensor_tensor(m2[:], c0_ps[:], m1[:], ALU.mult)
-        n2 = tile("n2", I, F32, tag="go_bf")
-        nc.vector.tensor_tensor(n2[:], n1[:], inv_sq[:], ALU.mult)
+        m2 = tile("m2", I, F32, tag="val_words")
+        nc.vector.tensor_tensor(m2[:], m1[:], n1[:], ALU.mult)
         m3 = tile("m3", I, F32)
-        nc.vector.tensor_tensor(m3[:], m2[:], inv_sq[:], ALU.mult)
-        nc.vector.tensor_tensor(placed[:].indirect(offsets[:]), m3[:], n2[:], ALU.mult)
+        nc.vector.tensor_tensor(m3[:], c0_ps[:], m2[:], ALU.mult)
+        nc.vector.tensor_tensor(placed[:].indirect(offsets[:]), m3[:], inv_4th[:], ALU.mult)
 
         first = 0
         for c, width in enumerate(OUT_WIDTHS):

@@ -3,7 +3,7 @@ from contextlib import ExitStack
 import concourse.mybir as mybir
 from concourse.masks import make_identity
 
-D, E, T, I, Q = 512, 512, 2048, 512, 128
+D, T, I, Q = 512, 2048, 512, 128
 FLOPS = 4 * 2 * D * Q * I
 
 F32 = mybir.dt.float32
@@ -18,8 +18,11 @@ ACT = mybir.ActivationFunctionType
 
 P = 128
 PACK = 4
+GROUP = 16
+QUADS = 4
+LINE = 4
 VALS_ROW = 4
-OUT_WIDTHS = (512, 512, 512, 512)
+OUT_CHUNK = 512
 
 
 def tile_attend_hvclippedratio_b_s_kernel(
@@ -33,7 +36,7 @@ def tile_attend_hvclippedratio_b_s_kernel(
         def tile(name, cols, dtype, tag=None):
             return sb.tile([P, cols], dtype, name=name, tag=tag or name, align_bytes=64)
 
-        offsets = sb.tile([P, I // 16], U16, name="offsets")
+        offsets = sb.tile([P, I // GROUP], U16, name="offsets")
         nc.sync.dma_start(offsets[:], offs)
 
         key_bytes = tile("key_bytes", T, U8)
@@ -48,10 +51,10 @@ def tile_attend_hvclippedratio_b_s_kernel(
             nc.sync.dma_start(raw[:], src.rearrange("(p j) w -> p j w", j=PACK))
             return raw
 
-        def load_scale_bytes(dst, src, first, quads):
-            for quad in quads:
+        def load_scale_bytes(plane, src, first):
+            for quad in range(QUADS):
                 rows = slice(32 * quad + first, 32 * quad + first + 4)
-                nc.sync.dma_start(dst[rows, :].bitcast(I32), src[0, 4 * quad : 4 * quad + 4, :].bitcast(I32))
+                nc.sync.dma_start(plane[rows, :].bitcast(I32), src[0, 4 * quad : 4 * quad + 4, :].bitcast(I32))
 
         def load_words(name, src):
             words = tile(name, T, U32)
@@ -65,7 +68,7 @@ def tile_attend_hvclippedratio_b_s_kernel(
 
         q2_raw = load_rows("q2", query2)
         q1_raw = load_rows("q1", query)
-        load_scale_bytes(key_bytes, keys_scales, 0, range(4))
+        load_scale_bytes(key_bytes, keys_scales, 0)
         key_words = load_words("key_words", keys_words)
         l2_col = load_column("l2_col", l2)
         floor_col = load_column("floor_col", floor)
@@ -74,7 +77,7 @@ def tile_attend_hvclippedratio_b_s_kernel(
         l1_col = load_column("l1_col", l1)
         dq_raw = load_rows("dq", dquery2)
         go_raw = load_rows("go", gout)
-        load_scale_bytes(val_bytes, vals_scales, VALS_ROW, range(4))
+        load_scale_bytes(val_bytes, vals_scales, VALS_ROW)
         val_words = load_words("val_words", vals_words)
         base_sb = tile("base_sb", T, F32)
         nc.sync.dma_start(base_sb[:], base)
@@ -84,42 +87,44 @@ def tile_attend_hvclippedratio_b_s_kernel(
 
         neg_l2 = sb.tile([P, 1], F32, name="neg_l2")
         nc.scalar.activation(neg_l2[:], l2_col[:], ACT.Copy, scale=-1.0)
+        neg_l12 = tile("neg_l12", 1, F32)
+        nc.scalar.activation(neg_l12[:], l1_col[:], ACT.Identity, bias=neg_l2[:], scale=-1.0)
         floor_sq = sb.tile([P, 1], F32, name="floor_sq")
         nc.scalar.activation(floor_sq[:], floor_col[:], ACT.Square)
 
-
-        def interleave(name, raw, on_scalar):
+        def interleave(name, raw, copy):
             grouped = sb.tile([P, Q, PACK], BF16, name=name + "_bf", align_bytes=64)
-            dst = grouped[:].rearrange("p (c i) j -> p c j i", i=4)
-            src = raw[:].rearrange("p j (c i) -> p c j i", i=4)
-            if on_scalar:
-                nc.scalar.copy(dst, src)
-            else:
-                nc.vector.tensor_copy(dst, src)
+            copy(
+                grouped[:].rearrange("p (c i) j -> p c j i", i=LINE),
+                raw[:].rearrange("p j (c i) -> p c j i", i=LINE),
+            )
             return grouped
 
         def quantize(name, grouped):
             codes = tile(name + "_codes", Q, U32)
-            scales = tile(name + "_scales", Q, U8)
-            nc.vector.quantize_mx(out=codes[:].bitcast(FP8X4), scales=scales[:], in_=grouped[:].rearrange("p w j -> p (w j)"))
-            return codes, scales
+            plane = tile(name + "_scales", Q, U8)
+            nc.vector.quantize_mx(
+                out=codes[:].bitcast(FP8X4), scales=plane[:], in_=grouped[:].rearrange("p w j -> p (w j)")
+            )
+            return codes, plane
 
         def gather(name, window, dtype, slots):
             picked = tile(name, slots.stop - slots.start, dtype)
-            nc.vector.tensor_copy(picked[:], window[:].indirect(offsets[:, slots.start // 16 : slots.stop // 16]))
+            entries = offsets[:, slots.start // GROUP : slots.stop // GROUP]
+            nc.vector.tensor_copy(picked[:], window[:].indirect(entries))
             return picked
 
-        def product(acc, rows, words, planes, start, stop):
+        def product(acc, rows, words, plane, start, stop):
             nc.tensor.matmul_mx(
                 out=acc, lhsT=rows[0][:].bitcast(FP8X4), lhsT_scale=rows[1][:],
-                rhs=words[:].bitcast(FP8X4), rhs_scale=planes, start=start, stop=stop,
+                rhs=words[:].bitcast(FP8X4), rhs_scale=plane, start=start, stop=stop,
             )
 
         every = slice(0, I)
         halves = [slice(0, I // 2), slice(I // 2, I)]
 
-        q2_bf = interleave("q2", q2_raw, False)
-        q1_bf = interleave("q1", q1_raw, True)
+        q2_bf = interleave("q2", q2_raw, nc.vector.tensor_copy)
+        q1_bf = interleave("q1", q1_raw, nc.scalar.copy)
         key_sc = gather("key_sc", key_bytes, U8, every)
         q2_mx = quantize("q2", q2_bf)
         q1_mx = quantize("q1", q1_bf)
@@ -138,22 +143,23 @@ def tile_attend_hvclippedratio_b_s_kernel(
             product(ab_ps[:, slots], q1_mx, key_w[h], key_sc[:, slots], False, True)
         pb_sq = tile("pb_sq", I, F32)
         nc.scalar.activation(pb_sq[:], pb[:], ACT.Square)
-        neg_l12 = tile("neg_l12", 1, F32)
-        nc.scalar.activation(neg_l12[:], l1_col[:], ACT.Identity, bias=neg_l2[:], scale=-1.0)
         pab = tile("pab", I, F32)
         nc.scalar.activation(pab[:], ab_ps[:], ACT.Exp, bias=neg_l12[:])
+
         size_ps = ps.tile([P, PACK, P], F32, name="size_ps", tag="b_ps1")
         for j in range(PACK):
             nc.tensor.transpose(size_ps[:, j, :], size_cols[:, j : j + 1].to_broadcast([P, P]), ident[:])
-        inv_abs = tile("inv_abs", I, F32, tag="neg_l12")
-        nc.scalar.activation(inv_abs[:], den_sq[:], ACT.Abs_reciprocal_sqrt)
-        inv_sq = tile("inv_sq", I, F32)
-        nc.scalar.activation(inv_sq[:], inv_abs[:], ACT.Square)
-        inv_4th = tile("inv_4th", I, F32)
-        nc.scalar.activation(inv_4th[:], inv_sq[:], ACT.Square)
 
-        dq_bf = interleave("dq", dq_raw, False)
-        go_bf = interleave("go", go_raw, False)
+        inv_abs = tile("inv_abs", I, F32, tag="neg_l12")
+        inv_sq = tile("inv_sq", I, F32)
+        inv_4th = tile("inv_4th", I, F32)
+        for slots in halves:
+            nc.scalar.activation(inv_abs[:, slots], den_sq[:, slots], ACT.Abs_reciprocal_sqrt)
+            nc.scalar.activation(inv_sq[:, slots], inv_abs[:, slots], ACT.Square)
+            nc.scalar.activation(inv_4th[:, slots], inv_sq[:, slots], ACT.Square)
+
+        dq_bf = interleave("dq", dq_raw, nc.vector.tensor_copy)
+        go_bf = interleave("go", go_raw, nc.vector.tensor_copy)
         dq_mx = quantize("dq", dq_bf)
         go_mx = quantize("go", go_bf)
         val_sc = gather("val_sc", val_bytes, U8, every)
@@ -164,23 +170,22 @@ def tile_attend_hvclippedratio_b_s_kernel(
         c0_ps = ps.tile([P, I], F32, name="c0_ps")
         product(c0_ps[:], go_mx, val_w, val_sc[VALS_ROW:P, :], True, True)
 
-        m1 = tile("m1", I, F32)
-        nc.vector.scalar_tensor_tensor(m1[:], tb_ps[:], 512.0, pab[:], ALU.mult, ALU.mult)
-        n1 = tile("n1", I, F32, tag="val_bytes")
+        factors = tile("factors", 2 * I, F32, tag="val_bytes")
+        diff_size, tb_pab = factors[:, :I], factors[:, I:]
         nc.vector.scalar_tensor_tensor(
-            n1[:].rearrange("p (n j) -> p n j", j=PACK), pb_sq[:].rearrange("p (n j) -> p n j", j=PACK), floor_sq[:],
-            size_ps[:].rearrange("p j n -> p n j"), ALU.subtract, ALU.mult,
+            diff_size.rearrange("p (n j) -> p n j", j=PACK), pb_sq[:].rearrange("p (n j) -> p n j", j=PACK),
+            floor_sq[:], size_ps[:].rearrange("p j n -> p n j"), ALU.subtract, ALU.mult,
         )
-        m2 = tile("m2", I, F32, tag="val_words")
-        nc.vector.tensor_tensor(m2[:], m1[:], n1[:], ALU.mult)
-        m3 = tile("m3", I, F32)
-        nc.vector.tensor_tensor(m3[:], c0_ps[:], m2[:], ALU.mult)
-        nc.vector.tensor_tensor(placed[:].indirect(offsets[:]), m3[:], inv_4th[:], ALU.mult)
+        nc.vector.scalar_tensor_tensor(tb_pab, tb_ps[:], 512.0, pab[:], ALU.mult, ALU.mult)
+        without_c0 = tile("without_c0", I, F32, tag="val_words")
+        nc.vector.tensor_tensor(without_c0[:], tb_pab, diff_size, ALU.mult)
+        numerator = tile("numerator", I, F32)
+        nc.vector.tensor_tensor(numerator[:], c0_ps[:], without_c0[:], ALU.mult)
 
-        first = 0
-        for c, width in enumerate(OUT_WIDTHS):
-            cols = slice(first, first + width)
-            first = first + width
-            res = tile("res%d" % c, width, F32)
+        nc.vector.tensor_tensor(placed[:].indirect(offsets[:]), numerator[:], inv_4th[:], ALU.mult)
+
+        for c in range(T // OUT_CHUNK):
+            cols = slice(c * OUT_CHUNK, (c + 1) * OUT_CHUNK)
+            res = tile("res%d" % c, OUT_CHUNK, F32)
             nc.vector.tensor_tensor(res[:], placed[:, cols], base_sb[:, cols], ALU.add)
             nc.sync.dma_start(out[:, cols], res[:])

from contextlib import ExitStack

import concourse.mybir as mybir
from concourse.masks import make_identity

D, T, I, Q = 512, 2048, 512, 128
FLOPS = 4 * 2 * D * Q * I

F32 = mybir.dt.float32
BF16 = mybir.dt.bfloat16
I32 = mybir.dt.int32
U32 = mybir.dt.uint32
U16 = mybir.dt.uint16
U8 = mybir.dt.uint8
FP8X4 = mybir.dt.float8_e4m3fn_x4
ALU = mybir.AluOpType
ACT = mybir.ActivationFunctionType

P = 128
PACK = 4
GROUP = 16
QUADS = 4
LINE = 4
VALS_ROW = 4
OUT_CHUNK = 512


def tile_attend_hvclippedratio_b_s_kernel(
    tc, query, query2, keys_words, keys_scales, l1, l2, floor, gout, vals_words, vals_scales, size, dquery2, base, offs, out
):
    nc = tc.nc
    with ExitStack() as ctx:
        sb = ctx.enter_context(tc.tile_pool(name="sb", bufs=1))
        ps = ctx.enter_context(tc.psum_pool(name="ps", bufs=1))

        def tile(name, cols, dtype, tag=None):
            return sb.tile([P, cols], dtype, name=name, tag=tag or name, align_bytes=64)

        offsets = sb.tile([P, I // GROUP], U16, name="offsets")
        nc.sync.dma_start(offsets[:], offs)

        key_bytes = tile("key_bytes", T, U8)
        val_bytes = tile("val_bytes", T, U8)
        nc.gpsimd.memset(key_bytes[:].bitcast(I32), 0)
        nc.gpsimd.memset(val_bytes[:].bitcast(I32), 0)
        placed = tile("placed", T, F32)
        nc.vector.memset(placed[:], 0.0)

        def load_rows(name, src):
            raw = sb.tile([P, PACK, Q], F32, name=name + "_raw")
            nc.sync.dma_start(raw[:], src.rearrange("(p j) w -> p j w", j=PACK))
            return raw

        def load_scale_bytes(plane, src, first):
            for quad in range(QUADS):
                rows = slice(32 * quad + first, 32 * quad + first + 4)
                nc.sync.dma_start(plane[rows, :].bitcast(I32), src[0, 4 * quad : 4 * quad + 4, :].bitcast(I32))

        def load_words(name, src):
            words = tile(name, T, U32)
            nc.sync.dma_start(words[:].bitcast(I32), src[0].rearrange("p n t -> p (n t)").bitcast(I32))
            return words

        def load_column(name, src):
            col = tile(name, 1, F32)
            nc.sync.dma_start(col[:], src)
            return col

        q2_raw = load_rows("q2", query2)
        q1_raw = load_rows("q1", query)
        load_scale_bytes(key_bytes, keys_scales, 0)
        key_words = load_words("key_words", keys_words)
        l2_col = load_column("l2_col", l2)
        floor_col = load_column("floor_col", floor)
        size_cols = sb.tile([P, PACK], F32, name="size_cols")
        nc.sync.dma_start(size_cols[:], size.rearrange("o (p j) -> (o p) j", j=PACK))
        l1_col = load_column("l1_col", l1)
        dq_raw = load_rows("dq", dquery2)
        go_raw = load_rows("go", gout)
        load_scale_bytes(val_bytes, vals_scales, VALS_ROW)
        val_words = load_words("val_words", vals_words)
        base_sb = tile("base_sb", T, F32)
        nc.sync.dma_start(base_sb[:], base)

        ident = tile("ident", P, F32)
        make_identity(nc, ident[:])

        neg_l2 = sb.tile([P, 1], F32, name="neg_l2")
        nc.scalar.activation(neg_l2[:], l2_col[:], ACT.Copy, scale=-1.0)
        neg_l12 = tile("neg_l12", 1, F32)
        nc.scalar.activation(neg_l12[:], l1_col[:], ACT.Identity, bias=neg_l2[:], scale=-1.0)
        floor_sq = sb.tile([P, 1], F32, name="floor_sq")
        nc.scalar.activation(floor_sq[:], floor_col[:], ACT.Square)

        def interleave(name, raw, copy):
            grouped = sb.tile([P, Q, PACK], BF16, name=name + "_bf", align_bytes=64)
            copy(
                grouped[:].rearrange("p (c i) j -> p c j i", i=LINE),
                raw[:].rearrange("p j (c i) -> p c j i", i=LINE),
            )
            return grouped

        def quantize(name, grouped):
            codes = tile(name + "_codes", Q, U32)
            plane = tile(name + "_scales", Q, U8)
            nc.vector.quantize_mx(
                out=codes[:].bitcast(FP8X4), scales=plane[:], in_=grouped[:].rearrange("p w j -> p (w j)")
            )
            return codes, plane

        def gather(name, window, dtype, slots):
            picked = tile(name, slots.stop - slots.start, dtype)
            entries = offsets[:, slots.start // GROUP : slots.stop // GROUP]
            nc.vector.tensor_copy(picked[:], window[:].indirect(entries))
            return picked

        def product(acc, rows, words, plane, start, stop):
            nc.tensor.matmul_mx(
                out=acc, lhsT=rows[0][:].bitcast(FP8X4), lhsT_scale=rows[1][:],
                rhs=words[:].bitcast(FP8X4), rhs_scale=plane, start=start, stop=stop,
            )

        every = slice(0, I)
        halves = [slice(0, I // 2), slice(I // 2, I)]

        q2_bf = interleave("q2", q2_raw, nc.vector.tensor_copy)
        q1_bf = interleave("q1", q1_raw, nc.scalar.copy)
        key_sc = gather("key_sc", key_bytes, U8, every)
        q2_mx = quantize("q2", q2_bf)
        q1_mx = quantize("q1", q1_bf)
        key_w = [gather("key_w%d" % h, key_words, U32, slots) for h, slots in enumerate(halves)]

        pb = tile("pb", I, F32)
        den_sq = tile("den_sq", I, F32)
        for h, slots in enumerate(halves):
            b_ps = ps.tile([P, I // 2], F32, name="b_ps%d" % h)
            product(b_ps[:], q2_mx, key_w[h], key_sc[:, slots], True, True)
            nc.scalar.activation(pb[:, slots], b_ps[:], ACT.Exp, bias=neg_l2[:])
            nc.scalar.activation(den_sq[:, slots], pb[:, slots], ACT.Square, bias=floor_col[:])
        ab_ps = ps.tile([P, I], F32, name="ab_ps")
        for h, slots in enumerate(halves):
            product(ab_ps[:, slots], q2_mx, key_w[h], key_sc[:, slots], True, False)
            product(ab_ps[:, slots], q1_mx, key_w[h], key_sc[:, slots], False, True)
        pb_sq = tile("pb_sq", I, F32)
        nc.scalar.activation(pb_sq[:], pb[:], ACT.Square)
        pab = tile("pab", I, F32)
        nc.scalar.activation(pab[:], ab_ps[:], ACT.Exp, bias=neg_l12[:])

        size_ps = ps.tile([P, PACK, P], F32, name="size_ps", tag="b_ps1")
        for j in range(PACK):
            nc.tensor.transpose(size_ps[:, j, :], size_cols[:, j : j + 1].to_broadcast([P, P]), ident[:])

        inv_abs = tile("inv_abs", I, F32, tag="neg_l12")
        inv_sq = tile("inv_sq", I, F32)
        inv_4th = tile("inv_4th", I, F32)
        for slots in halves:
            nc.scalar.activation(inv_abs[:, slots], den_sq[:, slots], ACT.Abs_reciprocal_sqrt)
            nc.scalar.activation(inv_sq[:, slots], inv_abs[:, slots], ACT.Square)
            nc.scalar.activation(inv_4th[:, slots], inv_sq[:, slots], ACT.Square)

        dq_bf = interleave("dq", dq_raw, nc.vector.tensor_copy)
        go_bf = interleave("go", go_raw, nc.vector.tensor_copy)
        dq_mx = quantize("dq", dq_bf)
        go_mx = quantize("go", go_bf)
        val_sc = gather("val_sc", val_bytes, U8, every)
        tb_ps = ps.tile([P, I], F32, name="tb_ps")
        for h, slots in enumerate(halves):
            product(tb_ps[:, slots], dq_mx, key_w[h], key_sc[:, slots], True, True)
        val_w = gather("val_w", val_words, U32, every)
        c0_ps = ps.tile([P, I], F32, name="c0_ps")
        product(c0_ps[:], go_mx, val_w, val_sc[VALS_ROW:P, :], True, True)

        factors = tile("factors", 2 * I, F32, tag="val_bytes")
        diff_size, tb_pab = factors[:, :I], factors[:, I:]
        nc.vector.scalar_tensor_tensor(
            diff_size.rearrange("p (n j) -> p n j", j=PACK), pb_sq[:].rearrange("p (n j) -> p n j", j=PACK),
            floor_sq[:], size_ps[:].rearrange("p j n -> p n j"), ALU.subtract, ALU.mult,
        )
        nc.vector.scalar_tensor_tensor(tb_pab, tb_ps[:], 512.0, pab[:], ALU.mult, ALU.mult)
        without_c0 = tile("without_c0", I, F32, tag="val_words")
        nc.vector.tensor_tensor(without_c0[:], tb_pab, diff_size, ALU.mult)
        numerator = tile("numerator", I, F32)
        nc.vector.tensor_tensor(numerator[:], c0_ps[:], without_c0[:], ALU.mult)

        nc.vector.tensor_tensor(placed[:].indirect(offsets[:]), numerator[:], inv_4th[:], ALU.mult)

        for c in range(T // OUT_CHUNK):
            cols = slice(c * OUT_CHUNK, (c + 1) * OUT_CHUNK)
            res = tile("res%d" % c, OUT_CHUNK, F32)
            nc.vector.tensor_tensor(res[:], placed[:, cols], base_sb[:, cols], ALU.add)
            nc.sync.dma_start(out[:, cols], res[:])
